import numpy as np, ml_dtypes
CORES = [51,54,179,182]
N = 4
QP = 128
def setup_inputs(rng):
    return {"q": rng.standard_normal((N, 128, QP), dtype=np.float32).astype(ml_dtypes.bfloat16), "k": rng.standard_normal((N, 128, 128), dtype=np.float32).astype(ml_dtypes.bfloat16), "v": rng.standard_normal((N, 128, 128), dtype=np.float32).astype(ml_dtypes.bfloat16), "b": (8 * rng.standard_normal((N, 128, N * QP), dtype=np.float32)).astype(ml_dtypes.bfloat16)}
def setup_inputs_big(rng):
    d = setup_inputs(rng)
    for k in ("q", "k", "v", "b"): d[k] = (d[k].astype(np.float32) * 1024.0).astype(d[k].dtype)
    return d
def setup_inputs_small(rng):
    d = setup_inputs(rng)
    for k in ("q", "k", "v", "b"): d[k] = (d[k].astype(np.float32) * (1 / 1024.0)).astype(d[k].dtype)
    return d
def setup_inputs_apart(rng):
    d = setup_inputs(rng)
    f = (10.0 ** rng.permutation(np.linspace(-1.5, 1.5, N))).astype(np.float32).reshape(N, 1, 1)
    for k in ("q", "k", "v", "b"): d[k] = (d[k].astype(np.float32) * f).astype(d[k].dtype)
    return d
def reference(q, k, v, b):
    Q, K, V, B = q.astype(np.float64), k.astype(np.float64), v.astype(np.float64), b.astype(np.float64)
    y = np.zeros((N, 128, QP))
    for r in range(N):
        for j in range(N):
            y[r] += V[j].T @ np.maximum(K[j].T @ Q[r] + B[r][:, QP * j:QP * j + QP], 0.0)
    return {"y": y.astype(ml_dtypes.bfloat16 if q.dtype != np.float64 else np.float64)}

@@ -1,0 +1,119 @@
+from concourse.mybir import AluOpType
+
+N = 4
+P = 128
+
+SCRATCH = {
+    "qs": ("sbuf", [P, P], "bfloat16"),
+    "bs": ("sbuf", [P, N * P], "bfloat16"),
+    "nb": ("sbuf", [P, N * P], "bfloat16"),
+    "zero": ("sbuf", [P, N * P], "bfloat16"),
+    "m": ("sbuf", [P, N * P], "bfloat16"),
+    "ysb": ("sbuf", [P, P], "bfloat16"),
+    "o": ("psum", [P, 512], "float32"),
+}
+for _j in range(N):
+    SCRATCH["kv%d" % _j] = ("sbuf", [P, 2 * P], "bfloat16")
+    SCRATCH["s%d" % _j] = ("psum", [P, 512], "float32")
+
+SEMAPHORES = (["ld_kv", "ld_q", "ld_b", "sent", "zs", "nbs", "so", "sy", "st"]
+              + ["arr%d" % j for j in range(N)] + ["ss%d" % j for j in range(N)] + ["sm%d" % j for j in range(N)])
+
+
+def _bits(mask):
+    return [e for e in range(16) if (mask >> e) & 1]
+
+
+def _mask(engines):
+    m = 0
+    for e in engines:
+        m |= 1 << e
+    return m
+
+
+def _same_chip(topo, a, b):
+    return topo.host(a) == topo.host(b) and topo.chip(a) == topo.chip(b)
+
+
+def _plan(core, cores, topo):
+    others = [c for c in cores if c != core]
+    far = [c for c in others if not _same_chip(topo, core, c)]
+    near = [c for c in others if _same_chip(topo, core, c)]
+    far.sort(key=lambda c: 0 if topo.die(c) != topo.die(core) else 1)
+    far_mask = 0
+    for c in far:
+        far_mask |= topo.mask(core, c)
+    plan = [(c, topo.mask(core, c)) for c in far]
+    for c in near:
+        free = [e for e in _bits(topo.mask(core, c)) if not (far_mask >> e) & 1]
+        plan.append((c, _mask(free) if free else topo.mask(core, c)))
+    return plan
+
+
+def rank_program(g, core, T, topo):
+    r = T.rank_of(core)
+    if r is None:
+        return
+    S = T.sem
+    cores = list(T.cores)
+    own = T["kv%d" % r]
+
+    g.sync.dma_start(own[:, 0:P], T.k[:]).then_inc(S.ld_kv, 16)
+    g.scalar.dma_start(own[:, P:2 * P], T.v[:]).then_inc(S.ld_kv, 16)
+    g.sync.dma_start(T.qs[:], T.q[:]).then_inc(S.ld_q, 16)
+    g.scalar.dma_start(T.bs[:], T.b[:]).then_inc(S.ld_b, 16)
+
+    g.wait_ge(S.ld_kv, 32)
+    left = 0
+    for dst, mask in _plan(core, cores, topo):
+        rid, pid = topo.addr(dst, core)
+        g.remote_dma(own[:], own[:], S["arr%d" % r], S.sent, pid, rid, mask)
+        left += len(_bits(mask))
+
+    near, far = [], []
+    for c in cores:
+        if c == core:
+            continue
+        plan = _plan(c, cores, topo)
+        pos = [i for i, (d, _) in enumerate(plan) if d == core][0]
+        item = (pos, T.rank_of(c), len(_bits(plan[pos][1])))
+        (near if _same_chip(topo, c, core) else far).append(item)
+    order = [(r, None)] + [(j, n) for _, j, n in sorted(near)] + [(j, n) for _, j, n in sorted(far)]
+
+    def blk(t, j):
+        return t[:, P * j:P * j + P]
+
+    v = g.vector
+    v.memset(T.zero[:], 0.0).then_inc(S.zs, 1)
+    v.wait_ge(S.zs, 1)
+    v.wait_ge(S.ld_b, 16)
+    v.tensor_tensor(T.nb[:], T.zero[:], T.bs[:], AluOpType.subtract).then_inc(S.nbs, 1)
+    v.wait_ge(S.nbs, 1)
+    for j, _ in order:
+        v.wait_ge(S["ss%d" % j], 1)
+        v.tensor_tensor(blk(T.m, j), T["s%d" % j][:, 0:P], blk(T.nb, j), AluOpType.max).then_inc(S["sm%d" % j], 1)
+    v.wait_ge(S.so, 1)
+    v.tensor_copy(T.ysb[:], T.o[:, 0:P]).then_inc(S.sy, 1)
+
+    t = g.tensor
+    t.wait_ge(S.ld_q, 16)
+    t.wait_ge(S.ld_b, 16)
+    for i, (j, n) in enumerate(order):
+        kv = T["kv%d" % j]
+        if n is None:
+            t.wait_ge(S.ld_kv, 32)
+        else:
+            t.wait_ge(S["arr%d" % j], n)
+        t.matmul(T["s%d" % j][:, 0:P], kv[:, 0:P], T.qs[:], True, True).then_inc(S["ss%d" % j], 1)
+        t.matmul(T.o[:, 0:P], kv[:, P:2 * P], blk(T.bs, j), i == 0, False)
+        t.wait_ge(S["sm%d" % j], 1)
+        last = i == len(order) - 1
+        mm = t.matmul(T.o[:, 0:P], kv[:, P:2 * P], blk(T.m, j), False, last)
+        if last:
+            mm.then_inc(S.so, 1)
+
+    g.sync.wait_ge(S.sy, 1)
+    g.sync.dma_start(T.y[:], T.ysb[:]).then_inc(S.st, 16)
+    g.sync.wait_ge(S.st, 16)
+
+    g.wait_ge(S.sent, left)

@@ -1,23 +1,27 @@
+from concourse.bass import DstId, RemoteDMATransfer
 from concourse.mybir import AluOpType
 
 N = 4
 P = 128
+H = P // 2
 
 SCRATCH = {
     "qs": ("sbuf", [P, P], "bfloat16"),
     "bs": ("sbuf", [P, N * P], "bfloat16"),
-    "nb": ("sbuf", [P, N * P], "bfloat16"),
-    "zero": ("sbuf", [P, N * P], "bfloat16"),
+    "ramp": ("sbuf", [P, P], "bfloat16"),
+    "ident": ("sbuf", [P, P], "bfloat16"),
     "m": ("sbuf", [P, N * P], "bfloat16"),
     "ysb": ("sbuf", [P, P], "bfloat16"),
-    "o": ("psum", [P, 512], "float32"),
+    "o0": ("psum", [P, 512], "float32"),
+    "o1": ("psum", [P, 512], "float32"),
 }
 for _j in range(N):
     SCRATCH["kv%d" % _j] = ("sbuf", [P, 2 * P], "bfloat16")
     SCRATCH["s%d" % _j] = ("psum", [P, 512], "float32")
 
-SEMAPHORES = (["ld_kv", "ld_q", "ld_b", "sent", "zs", "nbs", "so", "sy", "st"]
-              + ["arr%d" % j for j in range(N)] + ["ss%d" % j for j in range(N)] + ["sm%d" % j for j in range(N)])
+SEMAPHORES = (["ld_k", "ld_v", "ld_q", "ld_b", "sent", "sio", "sid", "so0", "so1", "sy", "st"]
+              + ["arr%d" % j for j in range(N)] + ["ark%d" % j for j in range(N)] + ["arv%d" % j for j in range(N)]
+              + ["ss%d" % j for j in range(N)] + ["sm%d" % j for j in range(N)])
 
 
 def _bits(mask):
@@ -40,14 +44,14 @@ def _plan(core, cores, topo):
     far = [c for c in others if not _same_chip(topo, core, c)]
     near = [c for c in others if _same_chip(topo, core, c)]
     far.sort(key=lambda c: 0 if topo.die(c) != topo.die(core) else 1)
-    far_mask = 0
+    far_mask = topo.mask(core, far[0])
     for c in far:
-        far_mask |= topo.mask(core, c)
-    plan = [(c, topo.mask(core, c)) for c in far]
-    for c in near:
-        free = [e for e in _bits(topo.mask(core, c)) if not (far_mask >> e) & 1]
-        plan.append((c, _mask(free) if free else topo.mask(core, c)))
-    return plan
+        far_mask &= topo.mask(core, c)
+    near_mask = topo.mask(core, near[0])
+    free = [e for e in _bits(near_mask) if not (far_mask >> e) & 1]
+    if free:
+        near_mask = _mask(free)
+    return far, far_mask, near, near_mask
 
 
 def rank_program(g, core, T, topo):
@@ -57,62 +61,88 @@ def rank_program(g, core, T, topo):
     S = T.sem
     cores = list(T.cores)
     own = T["kv%d" % r]
+    far, far_mask, near, near_mask = _plan(core, cores, topo)
 
-    g.sync.dma_start(own[:, 0:P], T.k[:]).then_inc(S.ld_kv, 16)
-    g.scalar.dma_start(own[:, P:2 * P], T.v[:]).then_inc(S.ld_kv, 16)
+    g.sync.dma_start(own[:, 0:P], T.k[:]).then_inc(S.ld_k, 16)
+    g.scalar.dma_start(own[:, P:2 * P], T.v[:]).then_inc(S.ld_v, 16)
     g.sync.dma_start(T.qs[:], T.q[:]).then_inc(S.ld_q, 16)
     g.scalar.dma_start(T.bs[:], T.b[:]).then_inc(S.ld_b, 16)
 
-    g.wait_ge(S.ld_kv, 32)
+    g.iota(T.ramp[:], [[-1, P]], 0, 1, allow_small_or_imprecise_dtypes=True).then_inc(S.sio, 1)
+    ids = []
+    for c in far:
+        rid, pid = topo.addr(c, core)
+        ids.append(DstId(rid=rid, pnc=pid))
     left = 0
-    for dst, mask in _plan(core, cores, topo):
-        rid, pid = topo.addr(dst, core)
-        g.remote_dma(own[:], own[:], S["arr%d" % r], S.sent, pid, rid, mask)
-        left += len(_bits(mask))
+    for lo, ld, name in ((0, S.ld_k, "ark%d"), (P, S.ld_v, "arv%d")):
+        part = own[:, lo:lo + P]
+        g.wait_ge(ld, 16)
+        g.remote_dma_fused([RemoteDMATransfer(dst_ids=ids, dma_engine_mask=far_mask, remote_sem=S[name % r],
+                                              srcs=[part], dsts=[part for _ in far], alu_op=0)], local_sem=S.sent)
+        left += len(_bits(far_mask))
+    for c in near:
+        rid, pid = topo.addr(c, core)
+        g.remote_dma(own[:], own[:], S["arr%d" % r], S.sent, pid, rid, near_mask)
+        left += len(_bits(near_mask))
 
-    near, far = [], []
-    for c in cores:
-        if c == core:
-            continue
-        plan = _plan(c, cores, topo)
-        pos = [i for i, (d, _) in enumerate(plan) if d == core][0]
-        item = (pos, T.rank_of(c), len(_bits(plan[pos][1])))
-        (near if _same_chip(topo, c, core) else far).append(item)
-    order = [(r, None)] + [(j, n) for _, j, n in sorted(near)] + [(j, n) for _, j, n in sorted(far)]
+    nears = [(T.rank_of(c), len(_bits(_plan(c, cores, topo)[3]))) for c in near]
+    fars = []
+    for c in far:
+        f, fm, _, _ = _plan(c, cores, topo)
+        fars.append((f.index(core), T.rank_of(c), len(_bits(fm))))
+    fars = [(j, n) for _, j, n in sorted(fars)]
+    order = [r] + [j for j, _ in nears] + [j for j, _ in fars]
 
     def blk(t, j):
         return t[:, P * j:P * j + P]
 
     v = g.vector
-    v.memset(T.zero[:], 0.0).then_inc(S.zs, 1)
-    v.wait_ge(S.zs, 1)
-    v.wait_ge(S.ld_b, 16)
-    v.tensor_tensor(T.nb[:], T.zero[:], T.bs[:], AluOpType.subtract).then_inc(S.nbs, 1)
-    v.wait_ge(S.nbs, 1)
-    for j, _ in order:
+    v.wait_ge(S.sio, 1)
+    v.tensor_scalar(T.ident[:], T.ramp[:], 0.0, None, AluOpType.is_equal).then_inc(S.sid, 1)
+    for j in order:
         v.wait_ge(S["ss%d" % j], 1)
-        v.tensor_tensor(blk(T.m, j), T["s%d" % j][:, 0:P], blk(T.nb, j), AluOpType.max).then_inc(S["sm%d" % j], 1)
-    v.wait_ge(S.so, 1)
-    v.tensor_copy(T.ysb[:], T.o[:, 0:P]).then_inc(S.sy, 1)
+        v.tensor_scalar(blk(T.m, j), T["s%d" % j][:, 0:P], 0.0, None, AluOpType.max).then_inc(S["sm%d" % j], 1)
+    v.wait_ge(S.so0, 1)
+    v.tensor_copy(T.ysb[:, 0:H], T.o0[:, 0:H]).then_inc(S.sy, 1)
+    v.wait_ge(S.so1, 1)
+    v.tensor_copy(T.ysb[:, H:P], T.o1[:, 0:H]).then_inc(S.sy, 1)
 
     t = g.tensor
-    t.wait_ge(S.ld_q, 16)
-    t.wait_ge(S.ld_b, 16)
-    for i, (j, n) in enumerate(order):
-        kv = T["kv%d" % j]
-        if n is None:
-            t.wait_ge(S.ld_kv, 32)
-        else:
-            t.wait_ge(S["arr%d" % j], n)
-        t.matmul(T["s%d" % j][:, 0:P], kv[:, 0:P], T.qs[:], True, True).then_inc(S["ss%d" % j], 1)
-        t.matmul(T.o[:, 0:P], kv[:, P:2 * P], blk(T.bs, j), i == 0, False)
-        t.wait_ge(S["sm%d" % j], 1)
-        last = i == len(order) - 1
-        mm = t.matmul(T.o[:, 0:P], kv[:, P:2 * P], blk(T.m, j), False, last)
-        if last:
-            mm.then_inc(S.so, 1)
 
-    g.sync.wait_ge(S.sy, 1)
+    def first(j):
+        t.matmul(T["s%d" % j][:, 0:P], T["kv%d" % j][:, 0:P], T.qs[:], False, True).then_inc(S["ss%d" % j], 1)
+
+    def second(j):
+        start, stop = j == order[0], j == order[-1]
+        for h, (o, so) in enumerate(((T.o0, S.so0), (T.o1, S.so1))):
+            mm = t.matmul(o[:, 0:H], T["kv%d" % j][:, P:2 * P], T.m[:, P * j + H * h:P * j + H * h + H], start, stop)
+            if stop:
+                mm.then_inc(so, 1)
+
+    t.wait_ge(S.sid, 1)
+    t.wait_ge(S.ld_b, 16)
+    for j in order:
+        t.matmul(T["s%d" % j][:, 0:P], T.ident[:], blk(T.bs, j), True, False)
+    t.wait_ge(S.ld_q, 16)
+    t.wait_ge(S.ld_k, 16)
+    first(r)
+    t.wait_ge(S.ld_v, 16)
+    t.wait_ge(S["sm%d" % r], 1)
+    second(r)
+    for j, n in nears:
+        t.wait_ge(S["arr%d" % j], n)
+        first(j)
+        t.wait_ge(S["sm%d" % j], 1)
+        second(j)
+    for j, n in fars:
+        t.wait_ge(S["ark%d" % j], n)
+        first(j)
+    for j, n in fars:
+        t.wait_ge(S["sm%d" % j], 1)
+        t.wait_ge(S["arv%d" % j], n)
+        second(j)
+
+    g.sync.wait_ge(S.sy, 2)
     g.sync.dma_start(T.y[:], T.ysb[:]).then_inc(S.st, 16)
     g.sync.wait_ge(S.st, 16)
 

from concourse.bass import DstId, RemoteDMATransfer
from concourse.mybir import AluOpType

N = 4
P = 128
H = P // 2

SCRATCH = {
    "qs": ("sbuf", [P, P], "bfloat16"),
    "bs": ("sbuf", [P, N * P], "bfloat16"),
    "ramp": ("sbuf", [P, P], "bfloat16"),
    "ident": ("sbuf", [P, P], "bfloat16"),
    "m": ("sbuf", [P, N * P], "bfloat16"),
    "ysb": ("sbuf", [P, P], "bfloat16"),
    "o0": ("psum", [P, 512], "float32"),
    "o1": ("psum", [P, 512], "float32"),
}
for _j in range(N):
    SCRATCH["kv%d" % _j] = ("sbuf", [P, 2 * P], "bfloat16")
    SCRATCH["s%d" % _j] = ("psum", [P, 512], "float32")

SEMAPHORES = (["ld_k", "ld_v", "ld_q", "ld_b", "sent", "sio", "sid", "so0", "so1", "sy", "st"]
              + ["arr%d" % j for j in range(N)] + ["ark%d" % j for j in range(N)] + ["arv%d" % j for j in range(N)]
              + ["ss%d" % j for j in range(N)] + ["sm%d" % j for j in range(N)])


def _bits(mask):
    return [e for e in range(16) if (mask >> e) & 1]


def _mask(engines):
    m = 0
    for e in engines:
        m |= 1 << e
    return m


def _same_chip(topo, a, b):
    return topo.host(a) == topo.host(b) and topo.chip(a) == topo.chip(b)


def _plan(core, cores, topo):
    others = [c for c in cores if c != core]
    far = [c for c in others if not _same_chip(topo, core, c)]
    near = [c for c in others if _same_chip(topo, core, c)]
    far.sort(key=lambda c: 0 if topo.die(c) != topo.die(core) else 1)
    far_mask = topo.mask(core, far[0])
    for c in far:
        far_mask &= topo.mask(core, c)
    near_mask = topo.mask(core, near[0])
    free = [e for e in _bits(near_mask) if not (far_mask >> e) & 1]
    if free:
        near_mask = _mask(free)
    return far, far_mask, near, near_mask


def rank_program(g, core, T, topo):
    r = T.rank_of(core)
    if r is None:
        return
    S = T.sem
    cores = list(T.cores)
    own = T["kv%d" % r]
    far, far_mask, near, near_mask = _plan(core, cores, topo)

    g.sync.dma_start(own[:, 0:P], T.k[:]).then_inc(S.ld_k, 16)
    g.scalar.dma_start(own[:, P:2 * P], T.v[:]).then_inc(S.ld_v, 16)
    g.sync.dma_start(T.qs[:], T.q[:]).then_inc(S.ld_q, 16)
    g.scalar.dma_start(T.bs[:], T.b[:]).then_inc(S.ld_b, 16)

    g.iota(T.ramp[:], [[-1, P]], 0, 1, allow_small_or_imprecise_dtypes=True).then_inc(S.sio, 1)
    ids = []
    for c in far:
        rid, pid = topo.addr(c, core)
        ids.append(DstId(rid=rid, pnc=pid))
    left = 0
    for lo, ld, name in ((0, S.ld_k, "ark%d"), (P, S.ld_v, "arv%d")):
        part = own[:, lo:lo + P]
        g.wait_ge(ld, 16)
        g.remote_dma_fused([RemoteDMATransfer(dst_ids=ids, dma_engine_mask=far_mask, remote_sem=S[name % r],
                                              srcs=[part], dsts=[part for _ in far], alu_op=0)], local_sem=S.sent)
        left += len(_bits(far_mask))
    for c in near:
        rid, pid = topo.addr(c, core)
        g.remote_dma(own[:], own[:], S["arr%d" % r], S.sent, pid, rid, near_mask)
        left += len(_bits(near_mask))

    nears = [(T.rank_of(c), len(_bits(_plan(c, cores, topo)[3]))) for c in near]
    fars = []
    for c in far:
        f, fm, _, _ = _plan(c, cores, topo)
        fars.append((f.index(core), T.rank_of(c), len(_bits(fm))))
    fars = [(j, n) for _, j, n in sorted(fars)]
    order = [r] + [j for j, _ in nears] + [j for j, _ in fars]

    def blk(t, j):
        return t[:, P * j:P * j + P]

    v = g.vector
    v.wait_ge(S.sio, 1)
    v.tensor_scalar(T.ident[:], T.ramp[:], 0.0, None, AluOpType.is_equal).then_inc(S.sid, 1)
    for j in order:
        v.wait_ge(S["ss%d" % j], 1)
        v.tensor_scalar(blk(T.m, j), T["s%d" % j][:, 0:P], 0.0, None, AluOpType.max).then_inc(S["sm%d" % j], 1)
    v.wait_ge(S.so0, 1)
    v.tensor_copy(T.ysb[:, 0:H], T.o0[:, 0:H]).then_inc(S.sy, 1)
    v.wait_ge(S.so1, 1)
    v.tensor_copy(T.ysb[:, H:P], T.o1[:, 0:H]).then_inc(S.sy, 1)

    t = g.tensor

    def first(j):
        t.matmul(T["s%d" % j][:, 0:P], T["kv%d" % j][:, 0:P], T.qs[:], False, True).then_inc(S["ss%d" % j], 1)

    def second(j):
        start, stop = j == order[0], j == order[-1]
        for h, (o, so) in enumerate(((T.o0, S.so0), (T.o1, S.so1))):
            mm = t.matmul(o[:, 0:H], T["kv%d" % j][:, P:2 * P], T.m[:, P * j + H * h:P * j + H * h + H], start, stop)
            if stop:
                mm.then_inc(so, 1)

    t.wait_ge(S.sid, 1)
    t.wait_ge(S.ld_b, 16)
    for j in order:
        t.matmul(T["s%d" % j][:, 0:P], T.ident[:], blk(T.bs, j), True, False)
    t.wait_ge(S.ld_q, 16)
    t.wait_ge(S.ld_k, 16)
    first(r)
    t.wait_ge(S.ld_v, 16)
    t.wait_ge(S["sm%d" % r], 1)
    second(r)
    for j, n in nears:
        t.wait_ge(S["arr%d" % j], n)
        first(j)
        t.wait_ge(S["sm%d" % j], 1)
        second(j)
    for j, n in fars:
        t.wait_ge(S["ark%d" % j], n)
        first(j)
    for j, n in fars:
        t.wait_ge(S["sm%d" % j], 1)
        t.wait_ge(S["arv%d" % j], n)
        second(j)

    g.sync.wait_ge(S.sy, 2)
    g.sync.dma_start(T.y[:], T.ysb[:]).then_inc(S.st, 16)
    g.sync.wait_ge(S.st, 16)

    g.wait_ge(S.sent, left)
